import numpy as np
import ml_dtypes


def mxq(x, axis, fmt="e4m3"):
    dtype, down = {"e4m3": (ml_dtypes.float8_e4m3fn, 7), "e5m2": (ml_dtypes.float8_e5m2, 14)}[fmt]
    v = np.moveaxis(np.asarray(x, np.float32).astype(ml_dtypes.bfloat16).astype(np.float64), axis, -1)
    blocks = v.reshape(v.shape[:-1] + (-1, 32))
    amax = np.abs(blocks).max(-1, keepdims=True)
    byte = np.maximum(np.where(amax > 0, np.frexp(amax)[1] - 1 + 127, 0) - down, 1)
    scale = np.exp2(byte - 127.0)
    codes = (blocks / scale).astype(np.float32).astype(dtype).astype(np.float64)
    return np.moveaxis((codes * scale).reshape(v.shape), -1, axis)


WIDE = False


def mx_kscale(k):
    if not WIDE:
        return np.ones(k)
    levels = np.array([10, -10, 5, -5, 0])
    if k % 512:
        return np.exp2(np.random.permutation(np.resize(levels, k // 32))).repeat(32)
    a = np.empty((k // 512, 16))
    for p in range(k // 512):
        a[p, :8] = np.random.permutation(np.resize(levels, 8))
        for g in range(8):
            far = levels[np.abs(levels - a[p, g]) >= 10]
            a[p, g + 8] = far[np.random.randint(len(far))]
    return np.exp2(a.ravel()).repeat(32)


def f64(x):
    return np.asarray(x).astype(np.float64)


def striped(idx):
    return np.tile(np.asarray(idx).reshape(-1, 16).T, (8, 1)).astype(np.uint16)


def unstriped(offs):
    return offs[:16].T.reshape(-1).astype(np.int64)


E2M1 = np.array([0.0, 0.5, 1.0, 1.5, 2.0, 3.0, 4.0, 6.0, -0.0, -0.5, -1.0, -1.5, -2.0, -3.0, -4.0, -6.0])


def pack_weight(w, fmt):
    k, n = w.shape
    w = f64(np.asarray(w, np.float32).astype(ml_dtypes.bfloat16)).reshape(k // 32, 32, n)
    amax = np.abs(w).max(1)
    if fmt == "e4m3":
        byte = np.frexp(amax)[1] - 1 + 127 - 7
    else:
        mant, ex = np.frexp(amax / 6.0)
        byte = np.where(mant > 0.5, ex, ex - 1) + 127
    byte = np.clip(np.where(amax > 0, byte, 1), 1, 254)
    scaled = (w * np.exp2(127.0 - byte)[:, None, :]).reshape(k, n).astype(np.float32)
    by_word = np.ascontiguousarray(scaled.reshape(k // 512, 128, 4, n).transpose(0, 1, 3, 2))
    if fmt == "e4m3":
        words = by_word.astype(ml_dtypes.float8_e4m3fn).view(np.uint8)
    else:
        c = by_word.astype(ml_dtypes.float4_e2m1fn).view(np.uint8) & 0xF
        words = (c[..., 0::2] | (c[..., 1::2] << 4)).reshape(k // 512, 128, 2 * n)
    return np.ascontiguousarray(words), np.ascontiguousarray(byte.astype(np.uint8).reshape(k // 512, 16, n))


def unpack_weight(words, scales, fmt):
    g, _, n = scales.shape
    words = np.ascontiguousarray(words).reshape(g, 128, n, -1)
    if fmt == "e4m3":
        vals = words.view(ml_dtypes.float8_e4m3fn).astype(np.float64)
    else:
        nib = np.empty((g, 128, n, 4), np.uint8)
        nib[..., 0::2] = words & 0xF
        nib[..., 1::2] = words >> 4
        vals = E2M1[nib]
    vals = vals * np.repeat(np.exp2(scales.astype(np.float64) - 127.0), 8, axis=1)[..., None]
    return vals.transpose(0, 1, 3, 2).reshape(g * 512, n)


D, E, T, I, Q, G = 512, 512, 2048, 512, 256, 32


def setup_inputs():
    n = np.random.standard_normal
    idx = np.random.permutation(T)[:I]
    fd = mx_kscale(D)
    fe = mx_kscale(E)
    keysp = pack_weight(n((D, T)) / fd[:, None], "e4m3")
    valsp = pack_weight(n((E, T)) / fe[:, None], "e4m3")
    return {
        "query": (n((D, Q)) * 0.7 / np.sqrt(D) * fd[:, None]).astype(np.float32),
        "keys_words": keysp[0],
        "keys_scales": keysp[1],
        "reserve": (np.random.uniform(1.0, 8.0, (I, 1))).astype(np.float32),
        "us": (np.random.uniform(0.5, 2.0, (I, 1))).astype(np.float32),
        "gout": (n((E, Q)) * 1 / np.sqrt(E) * fe[:, None]).astype(np.float32),
        "vals_words": valsp[0],
        "vals_scales": valsp[1],
        "old": (0.3 * n((I, Q))).astype(np.float32),
        "offs": striped(idx),
    }


def reference(query, keys_words, keys_scales, reserve, us, gout, vals_words, vals_scales, old, offs):
    idx = unstriped(offs)
    keysu = unpack_weight(keys_words, keys_scales, "e4m3")
    valsu = unpack_weight(vals_words, vals_scales, "e4m3")
    keysidxg = keysu[:, idx]
    queryq = mxq(f64(query), 0, "e4m3")
    a = keysidxg.T @ queryq
    p = np.exp(a)
    b = f64(us) / (p.reshape(I, G, Q // G).sum(axis=2) + f64(reserve))
    br = np.repeat(b, Q // G, axis=1)
    valsidxg = valsu[:, idx]
    goutq = mxq(f64(gout), 0, "e4m3")
    c0 = valsidxg.T @ goutq
    dbr = c0 * p
    db = dbr.reshape(I, G, Q // G).sum(axis=2)
    e1 = db * f64(us) / np.square(p.reshape(I, G, Q // G).sum(axis=2) + f64(reserve)) * (-1.0)
    r1 = np.repeat(e1, Q // G, axis=1)
    dp = c0 * br + r1
    da = dp * p
    y = da * 8.0 + f64(old)
    return y

@@ -1,0 +1,206 @@
+from contextlib import ExitStack
+
+import concourse.mybir as mybir
+from concourse.masks import make_identity
+
+F32 = mybir.dt.float32
+BF16 = mybir.dt.bfloat16
+I32 = mybir.dt.int32
+U32 = mybir.dt.uint32
+U16 = mybir.dt.uint16
+U8 = mybir.dt.uint8
+FP8X4 = mybir.dt.float8_e4m3fn_x4
+ALU = mybir.AluOpType
+ACT = mybir.ActivationFunctionType
+AX = mybir.AxisListType
+
+P = 128
+PACK = 4
+T = 2048
+SLOTS = 512
+Q = 256
+TEAM = 8
+G = Q // TEAM
+TILES = SLOTS // P
+HALVES = 2
+TPH = TILES // HALVES
+HS = SLOTS // HALVES
+FLOPS = 2 * 2 * 512 * SLOTS * Q
+
+
+def tile_attend_bteamshares_kernel(tc, query, keys_words, keys_scales, reserve, us, gout, vals_words, vals_scales, old, offs, out):
+    nc = tc.nc
+    with ExitStack() as ctx:
+        sb = ctx.enter_context(tc.tile_pool(name="sb", bufs=1))
+        reuse = ctx.enter_context(tc.tile_pool(name="reuse", bufs=1))
+        ps = ctx.enter_context(tc.psum_pool(name="ps", bufs=1))
+
+        offsets = sb.tile([P, SLOTS // 16], U16, name="offsets")
+        nc.sync.dma_start(offsets[:], offs)
+
+        def load_scales(engine, plane, scales, first):
+            for quad in range(4):
+                engine.dma_start(
+                    plane[32 * quad + first : 32 * quad + first + 4, :].bitcast(I32),
+                    scales[0, 4 * quad : 4 * quad + 4, :].bitcast(I32),
+                )
+
+        def load_words(name, words, tag):
+            t = sb.tile([P, T], I32, name=name, tag=tag, align_bytes=64)
+            nc.sync.dma_start(t[:], words[0].rearrange("p n t -> p (n t)").bitcast(I32))
+            return t
+
+        def load_rows(name, rows, tag):
+            t = sb.tile([P, PACK * Q], F32, name=name, tag=tag, align_bytes=64)
+            nc.sync.dma_start(t[:], rows.rearrange("(p j) w -> p (j w)", j=PACK))
+            return t
+
+        ks = sb.tile([P, T], U8, name="ks", align_bytes=64)
+        nc.vector.memset(ks[:].bitcast(I32), 0)
+        vs = reuse.tile([P, T], U8, name="vs", align_bytes=64, offset=0)
+        nc.vector.memset(vs[:].bitcast(I32), 0)
+        rows = sb.tile([P, P], F32, name="rows")
+        nc.gpsimd.memset(rows[:], 0.0)
+        ident = sb.tile([P, P], F32, name="ident")
+        make_identity(nc, ident[:])
+        q_raw = load_rows("q_raw", query, "first")
+        load_scales(nc.scalar, ks, keys_scales, 0)
+        load_scales(nc.gpsimd, vs, vals_scales, 4)
+        kw = load_words("kw", keys_words, "kw")
+        g_raw = load_rows("g_raw", gout, "second")
+        nc.gpsimd.dma_start(rows[0:TILES, :], us.rearrange("(r p) o -> r (p o)", p=P))
+        nc.gpsimd.dma_start(rows[TILES : 2 * TILES, :], reserve.rearrange("(r p) o -> r (p o)", p=P))
+        cols_ps = ps.tile([P, P], F32, name="cols_ps")
+        nc.tensor.transpose(cols_ps[:], rows[:], ident[:])
+        us8 = sb.tile([P, TILES], F32, name="us8")
+        res = sb.tile([P, TILES], F32, name="res")
+        nc.scalar.activation(us8[:], cols_ps[:, 0:TILES], ACT.Copy, scale=8.0)
+        nc.scalar.copy(res[:], cols_ps[:, TILES : 2 * TILES])
+
+        def interleave(engine_copy, name, raw):
+            t = sb.tile([P, Q * PACK], BF16, name=name, align_bytes=64)
+            engine_copy(
+                t[:].rearrange("p (c i t) -> p c t i", i=4, t=PACK),
+                raw[:].rearrange("p (t c i) -> p c t i", i=4, t=PACK),
+            )
+            return t
+
+        def quantize(name, grouped, scales):
+            codes = sb.tile([P, Q], U32, name=name + "_codes", align_bytes=64)
+            nc.vector.quantize_mx(out=codes[:].bitcast(FP8X4), scales=scales[:], in_=grouped[:])
+            return codes, scales
+
+        def gather_scales(name, plane):
+            t = sb.tile([P, SLOTS], U8, name=name, align_bytes=64)
+            nc.vector.tensor_copy(t[:], plane[:].indirect(offsets[:]))
+            return t
+
+        def gather_words(t, words, h):
+            cols = HS // 16
+            nc.vector.tensor_copy(t[:, h * HS : (h + 1) * HS], words[:].bitcast(U32).indirect(offsets[:, h * cols : (h + 1) * cols]))
+
+        def product(name, words_g, scales_g, first, codes, scales, h):
+            bank = ps.tile([P, TPH * Q], F32, name=name)
+            for r in range(TPH):
+                lo = h * HS + r * P
+                nc.tensor.matmul_mx(
+                    out=bank[:, r * Q : (r + 1) * Q],
+                    lhsT=words_g[:, lo : lo + P].bitcast(FP8X4),
+                    lhsT_scale=scales_g[first:P, lo : lo + P],
+                    rhs=codes[:].bitcast(FP8X4),
+                    rhs_scale=scales[:],
+                    start=True,
+                    stop=True,
+                )
+            return bank
+
+        def half(name):
+            return sb.tile([P, TPH * Q], F32, name=name)
+
+        def small(name):
+            return sb.tile([P, TPH * G], F32, name=name)
+
+        def teams(ap):
+            return ap.rearrange("p (n j) -> p n j", j=TEAM)
+
+        def spread(ap):
+            return ap.unsqueeze(2).to_broadcast([P, TPH * G, TEAM])
+
+        ksg = gather_scales("ksg", ks)
+        q_bf = interleave(nc.scalar.copy, "q_bf", q_raw)
+        vw = load_words("vw", vals_words, "first")
+        q_codes, q_scales = quantize("q", q_bf, sb.tile([P, Q], U8, name="q_scales", align_bytes=64))
+        p = []
+        kwg = sb.tile([P, SLOTS], U32, name="kwg", align_bytes=64)
+        for h in range(HALVES):
+            gather_words(kwg, kw, h)
+            a = product("a%d" % h, kwg, ksg, 0, q_codes, q_scales, h)
+            ph = half("p%d" % h)
+            nc.scalar.activation(ph[:], a[:], ACT.Exp)
+            p.append(ph)
+        vsg = gather_scales("vsg", vs)
+
+        def pool_copy(dst, src):
+            nc.gpsimd.tensor_scalar(dst, src, 1.0, 0.0, ALU.mult, ALU.add)
+
+        g_bf = interleave(pool_copy, "g_bf", g_raw)
+        old_sb = sb.tile([P, TILES * Q], F32, name="old_sb", tag="second", align_bytes=64)
+        nc.sync.dma_start(old_sb[:].rearrange("p (r q) -> p r q", r=TILES), old.rearrange("(r p) q -> p r q", p=P))
+        sums_all = reuse.tile([P, TILES * G], F32, name="sums_all", align_bytes=64, offset=0)
+        sums = [sums_all[:, h * TPH * G : (h + 1) * TPH * G] for h in range(HALVES)]
+        for h in range(HALVES):
+            nc.vector.tensor_reduce(sums[h], teams(p[h][:]), axis=AX.X, op=ALU.add)
+            if h == 0:
+                g_codes, g_scales = quantize("g", g_bf, reuse.tile([P, Q], U8, name="g_scales", align_bytes=64, offset=512))
+        rden, b8, w = [], [], []
+        for h in range(HALVES):
+            root = small("root%d" % h)
+            for r in range(TPH):
+                col = h * TPH + r
+                nc.scalar.activation(root[:, r * G : (r + 1) * G], sums[h][:, r * G : (r + 1) * G], ACT.Abs_reciprocal_sqrt, bias=res[:, col : col + 1])
+            mag = small("mag%d" % h)
+            nc.scalar.activation(mag[:], root[:], ACT.Square)
+            sgn = small("sgn%d" % h)
+            for r in range(TPH):
+                col = h * TPH + r
+                nc.scalar.activation(sgn[:, r * G : (r + 1) * G], sums[h][:, r * G : (r + 1) * G], ACT.Sign, bias=res[:, col : col + 1])
+            rd = small("rden%d" % h)
+            nc.gpsimd.tensor_tensor(rd[:], mag[:], sgn[:], ALU.mult)
+            b = small("b8_%d" % h)
+            for r in range(TPH):
+                col = h * TPH + r
+                nc.scalar.activation(b[:, r * G : (r + 1) * G], rd[:, r * G : (r + 1) * G], ACT.Copy, scale=us8[:, col : col + 1])
+            wh = half("w%d" % h)
+            nc.gpsimd.tensor_tensor(teams(wh[:]), teams(p[h][:]), spread(b[:]), ALU.mult)
+            rden.append(rd)
+            w.append(wh)
+        c0, dbr, db, t, u, y = [], [], [], [], [], []
+        vwg = reuse.tile([P, SLOTS], U32, name="vwg", align_bytes=64, offset=768)
+        for h in range(HALVES):
+            gather_words(vwg, vw, h)
+            c0.append(product("c%d" % h, vwg, vsg, 4, g_codes, g_scales, h))
+        for h in range(HALVES):
+            d = half("dbr%d" % h)
+            nc.vector.tensor_tensor(d[:], c0[h][:], p[h][:], ALU.mult)
+            dbr.append(d)
+        for h in range(HALVES):
+            d = small("db%d" % h)
+            nc.vector.tensor_reduce(d[:], teams(dbr[h][:]), axis=AX.X, op=ALU.add)
+            db.append(d)
+        for h in range(HALVES):
+            d = small("t%d" % h)
+            nc.vector.tensor_tensor(d[:], db[h][:], rden[h][:], ALU.mult)
+            t.append(d)
+        for h in range(HALVES):
+            d = half("u%d" % h)
+            nc.vector.tensor_tensor(teams(d[:]), teams(c0[h][:]), spread(t[h][:]), ALU.subtract)
+            u.append(d)
+        for h in range(HALVES):
+            d = half("y%d" % h)
+            nc.vector.tensor_tensor(d[:], u[h][:], w[h][:], ALU.mult)
+            y.append(d)
+        for r in range(TILES):
+            h, k = divmod(r, TPH)
+            d = sb.tile([P, Q], F32, name="o%d" % r)
+            nc.vector.tensor_tensor(d[:], y[h][:, k * Q : (k + 1) * Q], old_sb[:, r * Q : (r + 1) * Q], ALU.add)
+            (nc.sync if r % 2 == 0 else nc.scalar).dma_start(out[r * P : (r + 1) * P, :], d[:])

@@ -32,7 +32,6 @@ def tile_attend_bteamshares_kernel(tc, query, keys_words, keys_scales, reserve, 
     nc = tc.nc
     with ExitStack() as ctx:
         sb = ctx.enter_context(tc.tile_pool(name="sb", bufs=1))
-        reuse = ctx.enter_context(tc.tile_pool(name="reuse", bufs=1))
         ps = ctx.enter_context(tc.psum_pool(name="ps", bufs=1))
 
         offsets = sb.tile([P, SLOTS // 16], U16, name="offsets")
@@ -57,25 +56,28 @@ def tile_attend_bteamshares_kernel(tc, query, keys_words, keys_scales, reserve, 
 
         ks = sb.tile([P, T], U8, name="ks", align_bytes=64)
         nc.vector.memset(ks[:].bitcast(I32), 0)
-        vs = reuse.tile([P, T], U8, name="vs", align_bytes=64, offset=0)
+        vs = sb.tile([P, T], U8, name="vs", align_bytes=64)
         nc.vector.memset(vs[:].bitcast(I32), 0)
         rows = sb.tile([P, P], F32, name="rows")
         nc.gpsimd.memset(rows[:], 0.0)
-        ident = sb.tile([P, P], F32, name="ident")
-        make_identity(nc, ident[:])
-        q_raw = load_rows("q_raw", query, "first")
-        load_scales(nc.scalar, ks, keys_scales, 0)
-        load_scales(nc.gpsimd, vs, vals_scales, 4)
-        kw = load_words("kw", keys_words, "kw")
-        g_raw = load_rows("g_raw", gout, "second")
         nc.gpsimd.dma_start(rows[0:TILES, :], us.rearrange("(r p) o -> r (p o)", p=P))
         nc.gpsimd.dma_start(rows[TILES : 2 * TILES, :], reserve.rearrange("(r p) o -> r (p o)", p=P))
+        ident = sb.tile([P, P], F32, name="ident")
+        make_identity(nc, ident[:])
+        q_raw = load_rows("q_raw", query, "q_raw")
+        load_scales(nc.sync, ks, keys_scales, 0)
+        kw = load_words("kw", keys_words, "kw")
+        load_scales(nc.sync, vs, vals_scales, 4)
+        g_raw = load_rows("g_raw", gout, "g_raw")
+        vw = load_words("vw", vals_words, "vw")
+        old_sb = sb.tile([P, TILES * Q], F32, name="old_sb")
+        nc.sync.dma_start(old_sb[:].rearrange("p (r q) -> p r q", r=TILES), old.rearrange("(r p) q -> p r q", p=P))
         cols_ps = ps.tile([P, P], F32, name="cols_ps")
         nc.tensor.transpose(cols_ps[:], rows[:], ident[:])
         us8 = sb.tile([P, TILES], F32, name="us8")
-        res = sb.tile([P, TILES], F32, name="res")
+        res = sb.tile([P, TILES * G], F32, name="res")
         nc.scalar.activation(us8[:], cols_ps[:, 0:TILES], ACT.Copy, scale=8.0)
-        nc.scalar.copy(res[:], cols_ps[:, TILES : 2 * TILES])
+        nc.scalar.copy(res[:].rearrange("p (r g) -> p r g", g=G), cols_ps[:, TILES : 2 * TILES].unsqueeze(2).to_broadcast([P, TILES, G]))
 
         def interleave(engine_copy, name, raw):
             t = sb.tile([P, Q * PACK], BF16, name=name, align_bytes=64)
@@ -100,7 +102,7 @@ def tile_attend_bteamshares_kernel(tc, query, keys_words, keys_scales, reserve, 
             nc.vector.tensor_copy(t[:, h * HS : (h + 1) * HS], words[:].bitcast(U32).indirect(offsets[:, h * cols : (h + 1) * cols]))
 
         def product(name, words_g, scales_g, first, codes, scales, h):
-            bank = ps.tile([P, TPH * Q], F32, name=name)
+            bank = ps.tile([P, TPH * Q], F32, name=name, tag="half%d" % h)
             for r in range(TPH):
                 lo = h * HS + r * P
                 nc.tensor.matmul_mx(
@@ -128,79 +130,77 @@ def tile_attend_bteamshares_kernel(tc, query, keys_words, keys_scales, reserve, 
 
         ksg = gather_scales("ksg", ks)
         q_bf = interleave(nc.scalar.copy, "q_bf", q_raw)
-        vw = load_words("vw", vals_words, "first")
         q_codes, q_scales = quantize("q", q_bf, sb.tile([P, Q], U8, name="q_scales", align_bytes=64))
-        p = []
         kwg = sb.tile([P, SLOTS], U32, name="kwg", align_bytes=64)
+        by_member = sb.tile([P, TEAM, TILES * G], F32, name="by_member")
+        a = []
         for h in range(HALVES):
             gather_words(kwg, kw, h)
-            a = product("a%d" % h, kwg, ksg, 0, q_codes, q_scales, h)
+            a.append(product("a%d" % h, kwg, ksg, 0, q_codes, q_scales, h))
+            nc.scalar.activation(by_member[:, :, h * TPH * G : (h + 1) * TPH * G], a[h][:].rearrange("p (n j) -> p j n", j=TEAM), ACT.Exp)
+        p = []
+        for h in range(HALVES):
             ph = half("p%d" % h)
-            nc.scalar.activation(ph[:], a[:], ACT.Exp)
+            nc.scalar.activation(ph[:], a[h][:], ACT.Exp)
             p.append(ph)
+        warm = sb.tile([P, 1], F32, name="warm")
+        nc.scalar.activation(warm[:], p[1][:, 0:1], ACT.Abs_reciprocal_sqrt, bias=by_member[:, 0, P - 1 : P], scale=p[0][:, 0:1])
+        den_t = ps.tile([P, P], F32, name="den_t")
+        for j in range(TEAM):
+            nc.tensor.matmul(den_t[:], lhsT=by_member[:, j, :], rhs=ident[:], is_transpose=True, start=(j == 0), stop=False)
+        nc.tensor.matmul(den_t[:], lhsT=res[:], rhs=ident[:], is_transpose=True, start=False, stop=True)
         vsg = gather_scales("vsg", vs)
-
-        def pool_copy(dst, src):
-            nc.gpsimd.tensor_scalar(dst, src, 1.0, 0.0, ALU.mult, ALU.add)
-
-        g_bf = interleave(pool_copy, "g_bf", g_raw)
-        old_sb = sb.tile([P, TILES * Q], F32, name="old_sb", tag="second", align_bytes=64)
-        nc.sync.dma_start(old_sb[:].rearrange("p (r q) -> p r q", r=TILES), old.rearrange("(r p) q -> p r q", p=P))
-        sums_all = reuse.tile([P, TILES * G], F32, name="sums_all", align_bytes=64, offset=0)
-        sums = [sums_all[:, h * TPH * G : (h + 1) * TPH * G] for h in range(HALVES)]
-        for h in range(HALVES):
-            nc.vector.tensor_reduce(sums[h], teams(p[h][:]), axis=AX.X, op=ALU.add)
-            if h == 0:
-                g_codes, g_scales = quantize("g", g_bf, reuse.tile([P, Q], U8, name="g_scales", align_bytes=64, offset=512))
-        rden, b8, w = [], [], []
-        for h in range(HALVES):
-            root = small("root%d" % h)
-            for r in range(TPH):
-                col = h * TPH + r
-                nc.scalar.activation(root[:, r * G : (r + 1) * G], sums[h][:, r * G : (r + 1) * G], ACT.Abs_reciprocal_sqrt, bias=res[:, col : col + 1])
-            mag = small("mag%d" % h)
-            nc.scalar.activation(mag[:], root[:], ACT.Square)
-            sgn = small("sgn%d" % h)
-            for r in range(TPH):
-                col = h * TPH + r
-                nc.scalar.activation(sgn[:, r * G : (r + 1) * G], sums[h][:, r * G : (r + 1) * G], ACT.Sign, bias=res[:, col : col + 1])
-            rd = small("rden%d" % h)
-            nc.gpsimd.tensor_tensor(rd[:], mag[:], sgn[:], ALU.mult)
-            b = small("b8_%d" % h)
-            for r in range(TPH):
-                col = h * TPH + r
-                nc.scalar.activation(b[:, r * G : (r + 1) * G], rd[:, r * G : (r + 1) * G], ACT.Copy, scale=us8[:, col : col + 1])
-            wh = half("w%d" % h)
-            nc.gpsimd.tensor_tensor(teams(wh[:]), teams(p[h][:]), spread(b[:]), ALU.mult)
-            rden.append(rd)
-            w.append(wh)
-        c0, dbr, db, t, u, y = [], [], [], [], [], []
-        vwg = reuse.tile([P, SLOTS], U32, name="vwg", align_bytes=64, offset=768)
+        g_bf = interleave(nc.vector.tensor_copy, "g_bf", g_raw)
+        g_codes, g_scales = quantize("g", g_bf, sb.tile([P, Q], U8, name="g_scales", align_bytes=64))
+        c0, dbr, u, y, share = [], [], [], [], []
+        vwg = sb.tile([P, SLOTS], U32, name="vwg", align_bytes=64)
         for h in range(HALVES):
             gather_words(vwg, vw, h)
             c0.append(product("c%d" % h, vwg, vsg, 4, g_codes, g_scales, h))
+        root = sb.tile([P, P], F32, name="root")
+        sgn = sb.tile([P, P], F32, name="sgn")
+        mag = sb.tile([P, P], F32, name="mag")
+        rden_t = sb.tile([P, P], F32, name="rden_t", tag="vwg", align_bytes=64)
+        nc.scalar.activation(root[:], den_t[:], ACT.Abs_reciprocal_sqrt)
+        nc.scalar.activation(sgn[:], den_t[:], ACT.Sign)
+        nc.scalar.activation(mag[:], root[:], ACT.Square)
+        nc.gpsimd.tensor_tensor(rden_t[:], mag[:], sgn[:], ALU.mult)
+        rden = ps.tile([P, P], F32, name="rden")
+        nc.tensor.transpose(rden[:], rden_t[:], ident[:])
         for h in range(HALVES):
             d = half("dbr%d" % h)
             nc.vector.tensor_tensor(d[:], c0[h][:], p[h][:], ALU.mult)
             dbr.append(d)
+        db = sb.tile([P, TILES * G], F32, name="db")
+        HG = TPH * G
         for h in range(HALVES):
-            d = small("db%d" % h)
-            nc.vector.tensor_reduce(d[:], teams(dbr[h][:]), axis=AX.X, op=ALU.add)
-            db.append(d)
+            nc.vector.tensor_reduce(db[:, h * HG : (h + 1) * HG], teams(dbr[h][:]), axis=AX.X, op=ALU.add)
+        t = sb.tile([P, TILES * G], F32, name="t")
         for h in range(HALVES):
-            d = small("t%d" % h)
-            nc.vector.tensor_tensor(d[:], db[h][:], rden[h][:], ALU.mult)
-            t.append(d)
+            sh = half("share%d" % h)
+            nc.vector.tensor_tensor(teams(sh[:]), teams(p[h][:]), spread(rden[:, h * HG : (h + 1) * HG]), ALU.mult)
+            share.append(sh)
+            if h == 0:
+                nc.vector.tensor_tensor(t[:], db[:], rden[:], ALU.mult)
         for h in range(HALVES):
             d = half("u%d" % h)
-            nc.vector.tensor_tensor(teams(d[:]), teams(c0[h][:]), spread(t[h][:]), ALU.subtract)
+            nc.vector.tensor_tensor(teams(d[:]), teams(c0[h][:]), spread(t[:, h * HG : (h + 1) * HG]), ALU.subtract)
             u.append(d)
-        for h in range(HALVES):
-            d = half("y%d" % h)
-            nc.vector.tensor_tensor(d[:], u[h][:], w[h][:], ALU.mult)
-            y.append(d)
-        for r in range(TILES):
+
+        def scaled(r):
             h, k = divmod(r, TPH)
+            d = sb.tile([P, Q], F32, name="y%d" % r)
+            cols = slice(k * Q, (k + 1) * Q)
+            nc.vector.scalar_tensor_tensor(d[:], u[h][:, cols], us8[:, r : r + 1], share[h][:, cols], ALU.mult, ALU.mult)
+            y.append(d)
+
+        def finish(r):
             d = sb.tile([P, Q], F32, name="o%d" % r)
-            nc.vector.tensor_tensor(d[:], y[h][:, k * Q : (k + 1) * Q], old_sb[:, r * Q : (r + 1) * Q], ALU.add)
+            nc.vector.tensor_tensor(d[:], y[r][:], old_sb[:, r * Q : (r + 1) * Q], ALU.add)
             (nc.sync if r % 2 == 0 else nc.scalar).dma_start(out[r * P : (r + 1) * P, :], d[:])
+
+        scaled(0)
+        for r in range(1, TILES):
+            scaled(r)
+            finish(r - 1)
+        finish(TILES - 1)

@@ -38,10 +38,10 @@ def tile_attend_bteamshares_kernel(tc, query, keys_words, keys_scales, reserve, 
         nc.sync.dma_start(offsets[:], offs)
 
         def load_scales(engine, plane, scales, first):
-            for quad in range(4):
+            for row in range(4):
                 engine.dma_start(
-                    plane[32 * quad + first : 32 * quad + first + 4, :].bitcast(I32),
-                    scales[0, 4 * quad : 4 * quad + 4, :].bitcast(I32),
+                    plane[first + row : P : 32, :].bitcast(I32),
+                    scales[0, row:16:4, :].bitcast(I32),
                 )
 
         def load_words(name, words, tag):
@@ -166,6 +166,8 @@ def tile_attend_bteamshares_kernel(tc, query, keys_words, keys_scales, reserve, 
         nc.scalar.activation(mag[:], root[:], ACT.Square)
         nc.gpsimd.tensor_tensor(rden_t[:], mag[:], sgn[:], ALU.mult)
         rden = ps.tile([P, P], F32, name="rden")
+        rden_b = ps.tile([P, P], F32, name="rden_b")
+        nc.tensor.transpose(rden_b[:], rden_t[:], ident[:])
         nc.tensor.transpose(rden[:], rden_t[:], ident[:])
         for h in range(HALVES):
             d = half("dbr%d" % h)
@@ -176,12 +178,12 @@ def tile_attend_bteamshares_kernel(tc, query, keys_words, keys_scales, reserve, 
         for h in range(HALVES):
             nc.vector.tensor_reduce(db[:, h * HG : (h + 1) * HG], teams(dbr[h][:]), axis=AX.X, op=ALU.add)
         t = sb.tile([P, TILES * G], F32, name="t")
-        for h in range(HALVES):
-            sh = half("share%d" % h)
-            nc.vector.tensor_tensor(teams(sh[:]), teams(p[h][:]), spread(rden[:, h * HG : (h + 1) * HG]), ALU.mult)
-            share.append(sh)
-            if h == 0:
-                nc.vector.tensor_tensor(t[:], db[:], rden[:], ALU.mult)
+        rden_sb = small("rden_sb")
+        nc.scalar.copy(rden_sb[:], rden_b[:, 0:HG])
+        share = [half("share0"), half("share1")]
+        nc.gpsimd.tensor_tensor(teams(share[0][:]), teams(p[0][:]), spread(rden_sb[:]), ALU.mult)
+        nc.vector.tensor_tensor(t[:], db[:], rden[:], ALU.mult)
+        nc.vector.tensor_tensor(teams(share[1][:]), teams(p[1][:]), spread(rden[:, HG : 2 * HG]), ALU.mult)
         for h in range(HALVES):
             d = half("u%d" % h)
             nc.vector.tensor_tensor(teams(d[:]), teams(c0[h][:]), spread(t[:, h * HG : (h + 1) * HG]), ALU.subtract)

from contextlib import ExitStack

import concourse.mybir as mybir
from concourse.masks import make_identity

F32 = mybir.dt.float32
BF16 = mybir.dt.bfloat16
I32 = mybir.dt.int32
U32 = mybir.dt.uint32
U16 = mybir.dt.uint16
U8 = mybir.dt.uint8
FP8X4 = mybir.dt.float8_e4m3fn_x4
ALU = mybir.AluOpType
ACT = mybir.ActivationFunctionType
AX = mybir.AxisListType

P = 128
PACK = 4
T = 2048
SLOTS = 512
Q = 256
TEAM = 8
G = Q // TEAM
TILES = SLOTS // P
HALVES = 2
TPH = TILES // HALVES
HS = SLOTS // HALVES
FLOPS = 2 * 2 * 512 * SLOTS * Q


def tile_attend_bteamshares_kernel(tc, query, keys_words, keys_scales, reserve, us, gout, vals_words, vals_scales, old, offs, out):
    nc = tc.nc
    with ExitStack() as ctx:
        sb = ctx.enter_context(tc.tile_pool(name="sb", bufs=1))
        ps = ctx.enter_context(tc.psum_pool(name="ps", bufs=1))

        offsets = sb.tile([P, SLOTS // 16], U16, name="offsets")
        nc.sync.dma_start(offsets[:], offs)

        def load_scales(engine, plane, scales, first):
            for row in range(4):
                engine.dma_start(
                    plane[first + row : P : 32, :].bitcast(I32),
                    scales[0, row:16:4, :].bitcast(I32),
                )

        def load_words(name, words, tag):
            t = sb.tile([P, T], I32, name=name, tag=tag, align_bytes=64)
            nc.sync.dma_start(t[:], words[0].rearrange("p n t -> p (n t)").bitcast(I32))
            return t

        def load_rows(name, rows, tag):
            t = sb.tile([P, PACK * Q], F32, name=name, tag=tag, align_bytes=64)
            nc.sync.dma_start(t[:], rows.rearrange("(p j) w -> p (j w)", j=PACK))
            return t

        ks = sb.tile([P, T], U8, name="ks", align_bytes=64)
        nc.vector.memset(ks[:].bitcast(I32), 0)
        vs = sb.tile([P, T], U8, name="vs", align_bytes=64)
        nc.vector.memset(vs[:].bitcast(I32), 0)
        rows = sb.tile([P, P], F32, name="rows")
        nc.gpsimd.memset(rows[:], 0.0)
        nc.gpsimd.dma_start(rows[0:TILES, :], us.rearrange("(r p) o -> r (p o)", p=P))
        nc.gpsimd.dma_start(rows[TILES : 2 * TILES, :], reserve.rearrange("(r p) o -> r (p o)", p=P))
        ident = sb.tile([P, P], F32, name="ident")
        make_identity(nc, ident[:])
        q_raw = load_rows("q_raw", query, "q_raw")
        load_scales(nc.sync, ks, keys_scales, 0)
        kw = load_words("kw", keys_words, "kw")
        load_scales(nc.sync, vs, vals_scales, 4)
        g_raw = load_rows("g_raw", gout, "g_raw")
        vw = load_words("vw", vals_words, "vw")
        old_sb = sb.tile([P, TILES * Q], F32, name="old_sb")
        nc.sync.dma_start(old_sb[:].rearrange("p (r q) -> p r q", r=TILES), old.rearrange("(r p) q -> p r q", p=P))
        cols_ps = ps.tile([P, P], F32, name="cols_ps")
        nc.tensor.transpose(cols_ps[:], rows[:], ident[:])
        us8 = sb.tile([P, TILES], F32, name="us8")
        res = sb.tile([P, TILES * G], F32, name="res")
        nc.scalar.activation(us8[:], cols_ps[:, 0:TILES], ACT.Copy, scale=8.0)
        nc.scalar.copy(res[:].rearrange("p (r g) -> p r g", g=G), cols_ps[:, TILES : 2 * TILES].unsqueeze(2).to_broadcast([P, TILES, G]))

        def interleave(engine_copy, name, raw):
            t = sb.tile([P, Q * PACK], BF16, name=name, align_bytes=64)
            engine_copy(
                t[:].rearrange("p (c i t) -> p c t i", i=4, t=PACK),
                raw[:].rearrange("p (t c i) -> p c t i", i=4, t=PACK),
            )
            return t

        def quantize(name, grouped, scales):
            codes = sb.tile([P, Q], U32, name=name + "_codes", align_bytes=64)
            nc.vector.quantize_mx(out=codes[:].bitcast(FP8X4), scales=scales[:], in_=grouped[:])
            return codes, scales

        def gather_scales(name, plane):
            t = sb.tile([P, SLOTS], U8, name=name, align_bytes=64)
            nc.vector.tensor_copy(t[:], plane[:].indirect(offsets[:]))
            return t

        def gather_words(t, words, h):
            cols = HS // 16
            nc.vector.tensor_copy(t[:, h * HS : (h + 1) * HS], words[:].bitcast(U32).indirect(offsets[:, h * cols : (h + 1) * cols]))

        def product(name, words_g, scales_g, first, codes, scales, h):
            bank = ps.tile([P, TPH * Q], F32, name=name, tag="half%d" % h)
            for r in range(TPH):
                lo = h * HS + r * P
                nc.tensor.matmul_mx(
                    out=bank[:, r * Q : (r + 1) * Q],
                    lhsT=words_g[:, lo : lo + P].bitcast(FP8X4),
                    lhsT_scale=scales_g[first:P, lo : lo + P],
                    rhs=codes[:].bitcast(FP8X4),
                    rhs_scale=scales[:],
                    start=True,
                    stop=True,
                )
            return bank

        def half(name):
            return sb.tile([P, TPH * Q], F32, name=name)

        def small(name):
            return sb.tile([P, TPH * G], F32, name=name)

        def teams(ap):
            return ap.rearrange("p (n j) -> p n j", j=TEAM)

        def spread(ap):
            return ap.unsqueeze(2).to_broadcast([P, TPH * G, TEAM])

        ksg = gather_scales("ksg", ks)
        q_bf = interleave(nc.scalar.copy, "q_bf", q_raw)
        q_codes, q_scales = quantize("q", q_bf, sb.tile([P, Q], U8, name="q_scales", align_bytes=64))
        kwg = sb.tile([P, SLOTS], U32, name="kwg", align_bytes=64)
        by_member = sb.tile([P, TEAM, TILES * G], F32, name="by_member")
        a = []
        for h in range(HALVES):
            gather_words(kwg, kw, h)
            a.append(product("a%d" % h, kwg, ksg, 0, q_codes, q_scales, h))
            nc.scalar.activation(by_member[:, :, h * TPH * G : (h + 1) * TPH * G], a[h][:].rearrange("p (n j) -> p j n", j=TEAM), ACT.Exp)
        p = []
        for h in range(HALVES):
            ph = half("p%d" % h)
            nc.scalar.activation(ph[:], a[h][:], ACT.Exp)
            p.append(ph)
        warm = sb.tile([P, 1], F32, name="warm")
        nc.scalar.activation(warm[:], p[1][:, 0:1], ACT.Abs_reciprocal_sqrt, bias=by_member[:, 0, P - 1 : P], scale=p[0][:, 0:1])
        den_t = ps.tile([P, P], F32, name="den_t")
        for j in range(TEAM):
            nc.tensor.matmul(den_t[:], lhsT=by_member[:, j, :], rhs=ident[:], is_transpose=True, start=(j == 0), stop=False)
        nc.tensor.matmul(den_t[:], lhsT=res[:], rhs=ident[:], is_transpose=True, start=False, stop=True)
        vsg = gather_scales("vsg", vs)
        g_bf = interleave(nc.vector.tensor_copy, "g_bf", g_raw)
        g_codes, g_scales = quantize("g", g_bf, sb.tile([P, Q], U8, name="g_scales", align_bytes=64))
        c0, dbr, u, y, share = [], [], [], [], []
        vwg = sb.tile([P, SLOTS], U32, name="vwg", align_bytes=64)
        for h in range(HALVES):
            gather_words(vwg, vw, h)
            c0.append(product("c%d" % h, vwg, vsg, 4, g_codes, g_scales, h))
        root = sb.tile([P, P], F32, name="root")
        sgn = sb.tile([P, P], F32, name="sgn")
        mag = sb.tile([P, P], F32, name="mag")
        rden_t = sb.tile([P, P], F32, name="rden_t", tag="vwg", align_bytes=64)
        nc.scalar.activation(root[:], den_t[:], ACT.Abs_reciprocal_sqrt)
        nc.scalar.activation(sgn[:], den_t[:], ACT.Sign)
        nc.scalar.activation(mag[:], root[:], ACT.Square)
        nc.gpsimd.tensor_tensor(rden_t[:], mag[:], sgn[:], ALU.mult)
        rden = ps.tile([P, P], F32, name="rden")
        rden_b = ps.tile([P, P], F32, name="rden_b")
        nc.tensor.transpose(rden_b[:], rden_t[:], ident[:])
        nc.tensor.transpose(rden[:], rden_t[:], ident[:])
        for h in range(HALVES):
            d = half("dbr%d" % h)
            nc.vector.tensor_tensor(d[:], c0[h][:], p[h][:], ALU.mult)
            dbr.append(d)
        db = sb.tile([P, TILES * G], F32, name="db")
        HG = TPH * G
        for h in range(HALVES):
            nc.vector.tensor_reduce(db[:, h * HG : (h + 1) * HG], teams(dbr[h][:]), axis=AX.X, op=ALU.add)
        t = sb.tile([P, TILES * G], F32, name="t")
        rden_sb = small("rden_sb")
        nc.scalar.copy(rden_sb[:], rden_b[:, 0:HG])
        share = [half("share0"), half("share1")]
        nc.gpsimd.tensor_tensor(teams(share[0][:]), teams(p[0][:]), spread(rden_sb[:]), ALU.mult)
        nc.vector.tensor_tensor(t[:], db[:], rden[:], ALU.mult)
        nc.vector.tensor_tensor(teams(share[1][:]), teams(p[1][:]), spread(rden[:, HG : 2 * HG]), ALU.mult)
        for h in range(HALVES):
            d = half("u%d" % h)
            nc.vector.tensor_tensor(teams(d[:]), teams(c0[h][:]), spread(t[:, h * HG : (h + 1) * HG]), ALU.subtract)
            u.append(d)

        def scaled(r):
            h, k = divmod(r, TPH)
            d = sb.tile([P, Q], F32, name="y%d" % r)
            cols = slice(k * Q, (k + 1) * Q)
            nc.vector.scalar_tensor_tensor(d[:], u[h][:, cols], us8[:, r : r + 1], share[h][:, cols], ALU.mult, ALU.mult)
            y.append(d)

        def finish(r):
            d = sb.tile([P, Q], F32, name="o%d" % r)
            nc.vector.tensor_tensor(d[:], y[r][:], old_sb[:, r * Q : (r + 1) * Q], ALU.add)
            (nc.sync if r % 2 == 0 else nc.scalar).dma_start(out[r * P : (r + 1) * P, :], d[:])

        scaled(0)
        for r in range(1, TILES):
            scaled(r)
            finish(r - 1)
        finish(TILES - 1)
